import numpy as np
import ml_dtypes


def mxq(x, axis, fmt="e4m3"):
    dtype, down = {"e4m3": (ml_dtypes.float8_e4m3fn, 7), "e5m2": (ml_dtypes.float8_e5m2, 14)}[fmt]
    v = np.moveaxis(np.asarray(x, np.float32).astype(ml_dtypes.bfloat16).astype(np.float64), axis, -1)
    blocks = v.reshape(v.shape[:-1] + (-1, 32))
    amax = np.abs(blocks).max(-1, keepdims=True)
    byte = np.maximum(np.where(amax > 0, np.frexp(amax)[1] - 1 + 127, 0) - down, 1)
    scale = np.exp2(byte - 127.0)
    codes = (blocks / scale).astype(np.float32).astype(dtype).astype(np.float64)
    return np.moveaxis((codes * scale).reshape(v.shape), -1, axis)


WIDE = False


def mx_kscale(k):
    if not WIDE:
        return np.ones(k)
    levels = np.array([10, -10, 5, -5, 0])
    if k % 512:
        return np.exp2(np.random.permutation(np.resize(levels, k // 32))).repeat(32)
    a = np.empty((k // 512, 16))
    for p in range(k // 512):
        a[p, :8] = np.random.permutation(np.resize(levels, 8))
        for g in range(8):
            far = levels[np.abs(levels - a[p, g]) >= 10]
            a[p, g + 8] = far[np.random.randint(len(far))]
    return np.exp2(a.ravel()).repeat(32)


def f64(x):
    return np.asarray(x).astype(np.float64)


def striped(idx):
    return np.tile(idx.reshape(-1, 16).T, (8, 1)).astype(np.uint16)


def unstriped(offs):
    return offs[:16].T.reshape(-1).astype(np.int64)


def striped8(idx):
    return np.concatenate([x.reshape(-1, 16).T for x in idx]).astype(np.uint16)


def runs(offs, k):
    lists = np.stack([offs[16 * r : 16 * r + 16].T.reshape(-1) for r in range(8)]).astype(np.int64)
    return lists[np.arange(k) % 512 // 64]


def pack_weight(w):
    k, n = w.shape
    w = f64(np.asarray(w, np.float32).astype(ml_dtypes.bfloat16)).reshape(k // 32, 32, n)
    amax = np.abs(w).max(1)
    byte = np.clip(np.where(amax > 0, np.frexp(amax)[1] - 1 + 127 - 7, 1), 1, 254)
    scaled = (w * np.exp2(127.0 - byte)[:, None, :]).reshape(k, n).astype(np.float32)
    words = np.ascontiguousarray(scaled.reshape(k // 512, 128, 4, n).transpose(0, 1, 3, 2)).astype(ml_dtypes.float8_e4m3fn).view(np.uint8)
    return words, np.ascontiguousarray(byte.astype(np.uint8).reshape(k // 512, 16, n))


def unpack_weight(words, scales):
    g, p, n, _ = words.shape
    vals = np.ascontiguousarray(words).view(ml_dtypes.float8_e4m3fn).astype(np.float64) * np.repeat(np.exp2(scales.astype(np.float64) - 127.0), 8, axis=1)[..., None]
    return vals.transpose(0, 1, 3, 2).reshape(g * 512, n)

def planes(y):
    n, m = y.shape
    v = y.astype(np.float32).astype(ml_dtypes.bfloat16).astype(np.float64).reshape(n // 32, 32, m)
    top = np.abs(v).max(1)
    byte = np.clip(np.where(top > 0, np.frexp(top)[1] - 1 + 127 - 7, 1), 1, 254)
    codes = (v * np.exp2(127.0 - byte)[:, None, :]).reshape(n, m).astype(np.float32).astype(ml_dtypes.float8_e4m3fn).view(np.uint8)
    words = codes.reshape(n // 512, 128, 4, m).transpose(0, 1, 3, 2)
    return np.ascontiguousarray(words), np.ascontiguousarray(byte.astype(np.uint8).reshape(n // 512, 16, m))


K, T, S, N, H, W = 512, 2048, 256, 512, 512, 1024


def setup_inputs():
    n = np.random.standard_normal
    s = mx_kscale(K)[:, None]
    u = mx_kscale(H)
    packed_xT = pack_weight(n((K, T)) * s)
    packed_w1 = pack_weight(n((K, H)) / np.sqrt(K) / s)
    packed_w2 = pack_weight(n((K, H)) / np.sqrt(K) / s)
    packed_w3 = pack_weight(n((H, N)) / np.sqrt(2 * H) / u[:, None])
    packed_w4 = pack_weight(n((H, N)) / np.sqrt(2 * H) / u[:, None])
    return {
        "x_words": packed_xT[0],
        "x_scales": packed_xT[1],
        "w1_words": packed_w1[0],
        "w1_scales": packed_w1[1],
        "w2_words": packed_w2[0],
        "w2_scales": packed_w2[1],
        "gn": (np.random.uniform(0.5, 1.5, (H, 1)) * u[:, None]).astype(np.float32),
        "gm": (np.random.uniform(0.5, 1.5, (H, 1)) * u[:, None]).astype(np.float32),
        "w3_words": packed_w3[0],
        "w3_scales": packed_w3[1],
        "w4_words": packed_w4[0],
        "w4_scales": packed_w4[1],
        "offs": striped(np.random.permutation(T)[:S]),
        "hz": striped8(np.random.randint(0, T, (8, S))),
        "n1": striped(np.random.randint(0, S, W)),
        "n2": striped8(np.stack([np.random.permutation(S) for _ in range(8)])),
        "n3": striped8(np.stack([np.random.permutation(S) for _ in range(8)])),
        "n4": striped(np.random.permutation(S)),
        "n5": striped(np.random.permutation(S)),
    }


def reference(x_words, x_scales, w1_words, w1_scales, w2_words, w2_scales, gn, gm, w3_words, w3_scales, w4_words, w4_scales, offs, hz, n1, n2, n3, n4, n5):
    xq = unpack_weight(x_words, x_scales)[:, unstriped(offs)]
    y = unpack_weight(w1_words, w1_scales).T @ xq
    mb = y[:, unstriped(n1)]
    mn = mb.reshape(H, S, 4).min(axis=2)
    mx = mb.reshape(H, S, 4).max(axis=2)
    z = f64(gn) * (np.maximum(y, mn) - (0.5 * mx))
    x_hz = unpack_weight(x_words, x_scales)[np.arange(K)[:, None], runs(hz, K)]
    d = unpack_weight(w2_words, w2_scales).T @ x_hz
    z2 = f64(gm) * ((d * (d[np.arange(H)[:, None], runs(n2, H)])) * (np.tanh(d[np.arange(H)[:, None], runs(n3, H)])))
    h = unpack_weight(w3_words, w3_scales).T @ mxq(z, 0, "e4m3") + unpack_weight(w4_words, w4_scales).T @ mxq(z2, 0, "e4m3")
    st = np.maximum(h, h[:, unstriped(n4)])
    out_0 = st[:, unstriped(n5)] - (0.5 * h)
    return (out_0,) + planes(out_0)

@@ -1,0 +1,245 @@
+from contextlib import ExitStack
+
+import concourse.mybir as mybir
+
+K, T, S, N, H, W = 512, 2048, 256, 512, 512, 1024
+FLOPS = 4 * 2 * 512 * 512 * 256
+
+F32 = mybir.dt.float32
+BF16 = mybir.dt.bfloat16
+I32 = mybir.dt.int32
+U32 = mybir.dt.uint32
+U16 = mybir.dt.uint16
+U8 = mybir.dt.uint8
+FP8X4 = mybir.dt.float8_e4m3fn_x4
+ALU = mybir.AluOpType
+ACT = mybir.ActivationFunctionType
+
+P = 128
+PACK = 4
+HALF = S // 2
+Y_WINDOW = W + 8
+
+
+def tile_picked_hjoingmidcubehopb_none_po_kernel(
+    tc, x_words, x_scales, w1_words, w1_scales, w2_words, w2_scales, gn, gm, w3_words, w3_scales,
+    w4_words, w4_scales, offs, hz, n1, n2, n3, n4, n5, out_0, out_1, out_2,
+):
+    nc = tc.nc
+    with ExitStack() as ctx:
+        keep = ctx.enter_context(tc.tile_pool(name="keep", bufs=1))
+        psum = ctx.enter_context(tc.psum_pool(name="psum", bufs=1))
+
+        def sb(name, shape, dtype):
+            return keep.tile(shape, dtype, name=name, align_bytes=64)
+
+        def load_list(name, src):
+            t = keep.tile([P, src.shape[1]], U16, name=name)
+            nc.sync.dma_start(t[:], src)
+            return t
+
+        def words_of(src):
+            return src[0].rearrange("p c r -> p (c r)").bitcast(I32)
+
+        def load_words(queue, name, src):
+            t = sb(name, [P, src.shape[2]], I32)
+            queue.dma_start(t[:], words_of(src))
+            return t
+
+        def load_scales_all_rows(queue, name, src):
+            width = src.shape[2]
+            t = sb(name, [P, width], U8)
+            rows = src[0].bitcast(I32)
+            queue.dma_start(t[0:16, :].bitcast(I32), rows)
+            queue.dma_start(t[16:P, :].bitcast(I32), rows[2:16, :].unsqueeze(0).to_broadcast([8, 14, width // 4]))
+            return t
+
+        def deal(name, src, dtype):
+            t = sb(name, [P, H], dtype)
+            nc.vector.tensor_copy(t[:].rearrange("p (t m) -> p t m", t=PACK), src[:].rearrange("p (m t) -> p t m", t=PACK))
+            return t
+
+        def hcols(c):
+            return slice(c * HALF, (c + 1) * HALF)
+
+        def halves(lst, c):
+            return lst[:, c * (HALF // 16) : (c + 1) * (HALF // 16)]
+
+        def load_scale_rows(tile, first, src):
+            rows = src[0].bitcast(I32)
+            for q in range(4):
+                nc.sync.dma_start(tile[32 * q + first : 32 * q + first + 4, :].bitcast(I32), rows[4 * q : 4 * q + 4, :])
+
+        xs = sb("xs", [P, T], U8)
+        nc.vector.memset(xs[:].bitcast(I32), 0)
+        offs_t = load_list("offs_t", offs)
+        load_scale_rows(xs, 0, x_scales)
+        w1s_raw = load_scales_all_rows(nc.scalar, "w1s_raw", w1_scales)
+        xw = load_words(nc.sync, "xw", x_words)
+        w1w_raw = load_words(nc.sync, "w1w_raw", w1_words)
+        n1_t = load_list("n1_t", n1)
+        hz_t = load_list("hz_t", hz)
+
+        xs_offs = sb("xs_offs", [P, S], U8)
+        nc.vector.tensor_copy(xs_offs[:], xs[:].indirect(offs_t[:]))
+        for i in range(2):
+            nc.sync.dma_start(xs[16 + i : P : 32, :].bitcast(I32), x_scales[0].bitcast(I32)[2 + i : 16 : 4, :])
+        w1s = deal("w1s", w1s_raw, U8)
+        ws_raw = sb("ws_raw", [P, H], U8)
+        nc.vector.memset(ws_raw[:].bitcast(I32), 0)
+        y_win = [sb("y_win%d" % t, [P, Y_WINDOW], F32) for t in range(PACK)]
+        for t in range(PACK):
+            nc.vector.memset(y_win[t][:, S:], 0.0)
+
+        w2w_raw = load_words(nc.sync, "w2w_raw", w2_words)
+        w2s_raw = load_scales_all_rows(nc.sync, "w2s_raw", w2_scales)
+
+        xw_offs = sb("xw_offs", [P, S], U32)
+        nc.vector.tensor_copy(xw_offs[:], xw[:].bitcast(U32).indirect(offs_t[:]))
+        w1w = deal("w1w", w1w_raw, I32)
+        xw_hz = sb("xw_hz", [P, S], U32)
+        nc.vector.tensor_copy(xw_hz[:], xw[:].bitcast(U32).indirect(hz_t[:]))
+        xs_hz = sb("xs_hz", [P, S], U8)
+        nc.vector.tensor_copy(xs_hz[:], xs[:].indirect(hz_t[:]))
+        xs_hz_placed = sb("xs_hz_placed", [P, S], U8)
+        nc.vector.tensor_copy(xs_hz_placed[:].bitcast(I32), xs_hz[:].bitcast(I32))
+        for i in range(2):
+            nc.sync.dma_start(xs_hz_placed[2 + i : P : 32, :].bitcast(I32), xs_hz[16 + i : P : 32, :].bitcast(I32))
+
+        gm_t = sb("gm_t", [P, PACK], F32)
+        nc.sync.dma_start(gm_t[:], gm.rearrange("(p t) o -> p (t o)", t=PACK))
+        w3w_raw = load_words(nc.sync, "w3w_raw", w3_words)
+        w4w_raw = load_words(nc.sync, "w4w_raw", w4_words)
+        n2_t = load_list("n2_t", n2)
+        n3_t = load_list("n3_t", n3)
+        gn_t = sb("gn_t", [P, PACK], F32)
+        nc.sync.dma_start(gn_t[:], gn.rearrange("(p t) o -> p (t o)", t=PACK))
+        load_scale_rows(ws_raw, 0, w3_scales)
+        load_scale_rows(ws_raw, 4, w4_scales)
+        n4_t = load_list("n4_t", n4)
+        n5_t = load_list("n5_t", n5)
+
+        def cols(t):
+            return slice(t * P, (t + 1) * P)
+
+        members = [sb("members%d" % t, [P, S, 4], F32) for t in range(PACK)]
+        for t in range(PACK):
+            y_ps = psum.tile([P, S], F32, name="y_ps", tag="bank%d" % t)
+            nc.tensor.matmul_mx(y_ps[:], lhsT=w1w[:, cols(t)].bitcast(FP8X4), lhsT_scale=w1s[:, cols(t)],
+                                rhs=xw_offs[:].bitcast(FP8X4), rhs_scale=xs_offs[:], start=True, stop=True)
+            if t == 0:
+                nc.scalar.copy(y_win[t][:, :S], y_ps[:])
+            else:
+                nc.vector.tensor_copy(y_win[t][:, :S], y_ps[:])
+            nc.scalar.activation(members[t][:].rearrange("p j e -> p (j e)"), y_win[t][:].indirect(n1_t[:]), ACT.Copy)
+
+        w2w = deal("w2w", w2w_raw, I32)
+        w2s = deal("w2s", w2s_raw, U8)
+
+        d_ps = [psum.tile([P, 2, S], F32, name="d_ps%d" % b, tag="bank%d" % (4 + b)) for b in range(2)]
+        for t in range(PACK):
+            nc.tensor.matmul_mx(d_ps[t // 2][:, t % 2, :], lhsT=w2w[:, cols(t)].bitcast(FP8X4), lhsT_scale=w2s[:, cols(t)],
+                                rhs=xw_hz[:].bitcast(FP8X4), rhs_scale=xs_hz_placed[:], start=True, stop=True)
+
+        v = sb("v", [P, PACK, S], F32)
+        d_win = [sb("d_win%d" % t, [P, S], F32) for t in range(PACK)]
+        tanh_win = [sb("tanh_win%d" % t, [P, S], F32) for t in range(PACK)]
+        for t in range(PACK):
+            lo2 = sb("lo2_%d" % t, [P, S, 2], F32)
+            hi2 = sb("hi2_%d" % t, [P, S, 2], F32)
+            lo = sb("lo_%d" % t, [P, S], F32)
+            hi = sb("hi_%d" % t, [P, S], F32)
+            u = sb("u_%d" % t, [P, S], F32)
+            nc.vector.tensor_tensor(lo2[:], members[t][:, :, 0:2], members[t][:, :, 2:4], ALU.min)
+            nc.vector.tensor_tensor(hi2[:], members[t][:, :, 0:2], members[t][:, :, 2:4], ALU.max)
+            nc.vector.tensor_tensor(lo[:], lo2[:, :, 0], lo2[:, :, 1], ALU.min)
+            nc.vector.tensor_tensor(hi[:], hi2[:, :, 0], hi2[:, :, 1], ALU.max)
+            nc.vector.tensor_tensor(u[:], lo[:], y_win[t][:, :S], ALU.max)
+            nc.vector.tensor_scalar(d_win[t][:], d_ps[t // 2][:, t % 2, :], gm_t[:, t : t + 1], None, ALU.mult)
+            nc.vector.scalar_tensor_tensor(v[:, t, :], hi[:], -0.5, u[:], ALU.mult, ALU.add)
+
+        w3w = deal("w3w", w3w_raw, I32)
+        w4w = deal("w4w", w4w_raw, I32)
+        ws = deal("ws", ws_raw, U8)
+
+        def woven(ap):
+            return ap.rearrange("p (c i t) -> p c t i", i=4, t=PACK)
+
+        def planar(ap):
+            return ap.rearrange("p t (c i) -> p c t i", i=4)
+
+        z_bf = sb("z_bf", [P, S * PACK], BF16)
+        nc.vector.tensor_tensor(woven(z_bf[:]), planar(v[:]),
+                                gn_t[:].unsqueeze(1).unsqueeze(3).to_broadcast([P, S // 4, PACK, 4]), ALU.mult)
+        z_w = sb("z_w", [P, S], U32)
+        z_s = sb("z_s", [P, S], U8)
+        nc.vector.quantize_mx(z_w[:].bitcast(FP8X4), z_s[:], z_bf[:])
+
+        for t in range(PACK):
+            nc.scalar.activation(tanh_win[t][:], d_ps[t // 2][:, t % 2, :], ACT.Tanh)
+        d_n2 = sb("d_n2", [P, PACK, S], F32)
+        for t in range(PACK):
+            for c in range(2):
+                nc.scalar.activation(d_n2[:, t, c * HALF : (c + 1) * HALF], d_win[t][:].indirect(halves(n2_t, c)), ACT.Copy)
+        prod = sb("prod", [P, PACK, S], F32)
+        for b in range(2):
+            nc.vector.tensor_tensor(prod[:, 2 * b : 2 * b + 2, :], d_ps[b][:], d_n2[:, 2 * b : 2 * b + 2, :], ALU.mult)
+
+        first = psum.tile([P, PACK, HALF], F32, name="h_first", tag="bank0")
+        second = [psum.tile([P, 2, HALF], F32, name="h_second%d" % b, tag="bank%d" % (1 + b)) for b in range(2)]
+        h_ps = [[first[:, t, :] for t in range(PACK)], [second[t // 2][:, t % 2, :] for t in range(PACK)]]
+        per_bank = (4, 2)
+        for c in range(2):
+            for t in range(PACK):
+                nc.tensor.matmul_mx(h_ps[c][t], lhsT=w3w[:, cols(t)].bitcast(FP8X4), lhsT_scale=ws[:, cols(t)],
+                                    rhs=z_w[:, hcols(c)].bitcast(FP8X4), rhs_scale=z_s[:, hcols(c)],
+                                    start=(t % per_bank[c] == 0), stop=False)
+        for c in range(2):
+            tanh_n3 = sb("tanh_n3_%d" % c, [P, PACK, HALF], F32)
+            for t in range(PACK):
+                nc.scalar.activation(tanh_n3[:, t, :], tanh_win[t][:].indirect(halves(n3_t, c)), ACT.Copy)
+            z2_bf = sb("z2_bf%d" % c, [P, HALF * PACK], BF16)
+            nc.vector.tensor_tensor(woven(z2_bf[:]), planar(prod[:, :, hcols(c)]), planar(tanh_n3[:]), ALU.mult)
+            z2_w = sb("z2_w%d" % c, [P, HALF], U32)
+            z2_s = sb("z2_s%d" % c, [P, HALF], U8)
+            nc.vector.quantize_mx(z2_w[:].bitcast(FP8X4), z2_s[:], z2_bf[:])
+            for t in range(PACK):
+                nc.tensor.matmul_mx(h_ps[c][t], lhsT=w4w[:, cols(t)].bitcast(FP8X4), lhsT_scale=ws[4:P, cols(t)],
+                                    rhs=z2_w[:].bitcast(FP8X4), rhs_scale=z2_s[:],
+                                    start=False, stop=(t % per_bank[c] == per_bank[c] - 1))
+
+        h = sb("h", [P, PACK, S], F32)
+        nc.scalar.copy(h[:, :, hcols(0)], first[:])
+        nc.scalar.copy(h[:, 0:2, hcols(1)], second[0][:])
+        nc.vector.tensor_copy(h[:, 2:4, hcols(1)], second[1][:])
+        h_n4 = sb("h_n4", [P, PACK, S], F32)
+        st = sb("st", [P, PACK, S], F32)
+        st_n5 = sb("st_n5", [P, PACK, S], F32)
+        res = sb("res", [P, PACK, S], F32)
+        out_rows = out_0.rearrange("(p t) j -> p t j", t=PACK)
+        order = (0, 2, 1, 3)
+        for t in order:
+            for c in range(2):
+                if t < 2:
+                    nc.scalar.activation(h_n4[:, t, hcols(c)], h[:, t, :].indirect(halves(n4_t, c)), ACT.Copy)
+                else:
+                    nc.vector.tensor_copy(h_n4[:, t, hcols(c)], h[:, t, :].indirect(halves(n4_t, c)))
+            nc.vector.tensor_tensor(st[:, t, :], h_n4[:, t, :], h[:, t, :], ALU.max)
+        for t in order:
+            for c in range(2):
+                nc.scalar.activation(st_n5[:, t, hcols(c)], st[:, t, :].indirect(halves(n5_t, c)), ACT.Copy)
+            pieces = (hcols(0), hcols(1)) if t == order[-1] else (slice(0, S),)
+            for piece in pieces:
+                nc.vector.scalar_tensor_tensor(res[:, t, piece], h[:, t, piece], -0.5, st_n5[:, t, piece], ALU.mult, ALU.add)
+            nc.sync.dma_start(out_rows[:, t, :], res[:, t, :])
+        res_w = sb("res_w", [P, S], I32)
+        res_s = sb("res_s", [P, S], U8)
+        res_bf = [sb("res_bf%d" % c, [P, HALF * PACK], BF16) for c in range(2)]
+        for c in range(2):
+            nc.vector.tensor_copy(woven(res_bf[c][:]), planar(res[:, :, hcols(c)]))
+        for c in range(2):
+            nc.vector.quantize_mx(res_w[:, hcols(c)].bitcast(FP8X4), res_s[:, hcols(c)], res_bf[c][:])
+            nc.sync.dma_start(words_of(out_1)[:, hcols(c)], res_w[:, hcols(c)])
+        for q in range(4):
+            queue = nc.scalar if q % 2 == 0 else nc.sync
+            queue.dma_start(out_2[0].bitcast(I32)[4 * q : 4 * q + 4, :], res_s[32 * q : 32 * q + 4, :].bitcast(I32))

@@ -18,7 +18,7 @@ ACT = mybir.ActivationFunctionType
 P = 128
 PACK = 4
 HALF = S // 2
-Y_WINDOW = W + 8
+Y_WINDOW = W // 2 + 8
 
 
 def tile_picked_hjoingmidcubehopb_none_po_kernel(
@@ -46,18 +46,23 @@ def tile_picked_hjoingmidcubehopb_none_po_kernel(
             queue.dma_start(t[:], words_of(src))
             return t
 
-        def load_scales_all_rows(queue, name, src):
-            width = src.shape[2]
-            t = sb(name, [P, width], U8)
-            rows = src[0].bitcast(I32)
-            queue.dma_start(t[0:16, :].bitcast(I32), rows)
-            queue.dma_start(t[16:P, :].bitcast(I32), rows[2:16, :].unsqueeze(0).to_broadcast([8, 14, width // 4]))
-            return t
+        def load_first_rows(queue, tile, src):
+            queue.dma_start(tile[0:16, :].bitcast(I32), src[0].bitcast(I32))
 
-        def deal(name, src, dtype):
-            t = sb(name, [P, H], dtype)
-            nc.vector.tensor_copy(t[:].rearrange("p (t m) -> p t m", t=PACK), src[:].rearrange("p (m t) -> p t m", t=PACK))
-            return t
+        def load_other_rows(queue, tile, src):
+            rows = src[0].bitcast(I32)
+            queue.dma_start(tile[16:P, :].bitcast(I32), rows[2:16, :].unsqueeze(0).to_broadcast([8, 14, rows.shape[1]]))
+
+        def deal(name, src, dtype, steps=(PACK,)):
+            tile = sb(name, [P, H], dtype)
+            run = 4 if dtype == I32 else 16
+            dst = tile[:].rearrange("p (t c i) -> p c t i", t=PACK, i=run)
+            org = src[:].rearrange("p (c i t) -> p c t i", t=PACK, i=run)
+            first = 0
+            for step in steps:
+                nc.vector.tensor_copy(dst[:, :, first : first + step, :], org[:, :, first : first + step, :])
+                first = first + step
+            return tile
 
         def hcols(c):
             return slice(c * HALF, (c + 1) * HALF)
@@ -65,26 +70,29 @@ def tile_picked_hjoingmidcubehopb_none_po_kernel(
         def halves(lst, c):
             return lst[:, c * (HALF // 16) : (c + 1) * (HALF // 16)]
 
-        def load_scale_rows(tile, first, src):
+        def load_scale_rows(queue, tile, first, src):
             rows = src[0].bitcast(I32)
             for q in range(4):
-                nc.sync.dma_start(tile[32 * q + first : 32 * q + first + 4, :].bitcast(I32), rows[4 * q : 4 * q + 4, :])
+                queue.dma_start(tile[32 * q + first : 32 * q + first + 4, :].bitcast(I32), rows[4 * q : 4 * q + 4, :])
 
         xs = sb("xs", [P, T], U8)
         nc.vector.memset(xs[:].bitcast(I32), 0)
         offs_t = load_list("offs_t", offs)
-        load_scale_rows(xs, 0, x_scales)
-        w1s_raw = load_scales_all_rows(nc.scalar, "w1s_raw", w1_scales)
         xw = load_words(nc.sync, "xw", x_words)
+        load_scale_rows(nc.sync, xs, 0, x_scales)
+        w1s_raw = sb("w1s_raw", [P, H], U8)
+        load_first_rows(nc.sync, w1s_raw, w1_scales)
+        load_other_rows(nc.sync, w1s_raw, w1_scales)
         w1w_raw = load_words(nc.sync, "w1w_raw", w1_words)
         n1_t = load_list("n1_t", n1)
         hz_t = load_list("hz_t", hz)
 
+        xw_offs = sb("xw_offs", [P, S], U32)
+        nc.vector.tensor_copy(xw_offs[:], xw[:].bitcast(U32).indirect(offs_t[:]))
         xs_offs = sb("xs_offs", [P, S], U8)
         nc.vector.tensor_copy(xs_offs[:], xs[:].indirect(offs_t[:]))
         for i in range(2):
             nc.sync.dma_start(xs[16 + i : P : 32, :].bitcast(I32), x_scales[0].bitcast(I32)[2 + i : 16 : 4, :])
-        w1s = deal("w1s", w1s_raw, U8)
         ws_raw = sb("ws_raw", [P, H], U8)
         nc.vector.memset(ws_raw[:].bitcast(I32), 0)
         y_win = [sb("y_win%d" % t, [P, Y_WINDOW], F32) for t in range(PACK)]
@@ -92,11 +100,12 @@ def tile_picked_hjoingmidcubehopb_none_po_kernel(
             nc.vector.memset(y_win[t][:, S:], 0.0)
 
         w2w_raw = load_words(nc.sync, "w2w_raw", w2_words)
-        w2s_raw = load_scales_all_rows(nc.sync, "w2s_raw", w2_scales)
+        w2s_raw = sb("w2s_raw", [P, H], U8)
+        load_first_rows(nc.sync, w2s_raw, w2_scales)
+        load_other_rows(nc.sync, w2s_raw, w2_scales)
 
-        xw_offs = sb("xw_offs", [P, S], U32)
-        nc.vector.tensor_copy(xw_offs[:], xw[:].bitcast(U32).indirect(offs_t[:]))
-        w1w = deal("w1w", w1w_raw, I32)
+        w1s = deal("w1s", w1s_raw, U8, (1, 3))
+        w1w = deal("w1w", w1w_raw, I32, (1, 3))
         xw_hz = sb("xw_hz", [P, S], U32)
         nc.vector.tensor_copy(xw_hz[:], xw[:].bitcast(U32).indirect(hz_t[:]))
         xs_hz = sb("xs_hz", [P, S], U8)
@@ -114,8 +123,8 @@ def tile_picked_hjoingmidcubehopb_none_po_kernel(
         n3_t = load_list("n3_t", n3)
         gn_t = sb("gn_t", [P, PACK], F32)
         nc.sync.dma_start(gn_t[:], gn.rearrange("(p t) o -> p (t o)", t=PACK))
-        load_scale_rows(ws_raw, 0, w3_scales)
-        load_scale_rows(ws_raw, 4, w4_scales)
+        load_scale_rows(nc.sync, ws_raw, 0, w3_scales)
+        load_scale_rows(nc.sync, ws_raw, 4, w4_scales)
         n4_t = load_list("n4_t", n4)
         n5_t = load_list("n5_t", n5)
 
@@ -127,11 +136,13 @@ def tile_picked_hjoingmidcubehopb_none_po_kernel(
             y_ps = psum.tile([P, S], F32, name="y_ps", tag="bank%d" % t)
             nc.tensor.matmul_mx(y_ps[:], lhsT=w1w[:, cols(t)].bitcast(FP8X4), lhsT_scale=w1s[:, cols(t)],
                                 rhs=xw_offs[:].bitcast(FP8X4), rhs_scale=xs_offs[:], start=True, stop=True)
-            if t == 0:
+            if t < 2:
                 nc.scalar.copy(y_win[t][:, :S], y_ps[:])
             else:
                 nc.vector.tensor_copy(y_win[t][:, :S], y_ps[:])
-            nc.scalar.activation(members[t][:].rearrange("p j e -> p (j e)"), y_win[t][:].indirect(n1_t[:]), ACT.Copy)
+            for c in range(2):
+                nc.scalar.activation(members[t][:, hcols(c), :].rearrange("p j e -> p (j e)"),
+                                     y_win[t][:].indirect(n1_t[:, c * 32 : (c + 1) * 32]), ACT.Copy)
 
         w2w = deal("w2w", w2w_raw, I32)
         w2s = deal("w2s", w2s_raw, U8)
@@ -141,7 +152,7 @@ def tile_picked_hjoingmidcubehopb_none_po_kernel(
             nc.tensor.matmul_mx(d_ps[t // 2][:, t % 2, :], lhsT=w2w[:, cols(t)].bitcast(FP8X4), lhsT_scale=w2s[:, cols(t)],
                                 rhs=xw_hz[:].bitcast(FP8X4), rhs_scale=xs_hz_placed[:], start=True, stop=True)
 
-        v = sb("v", [P, PACK, S], F32)
+        v = keep.tile([P, PACK, S], F32, name="v", tag="planes", align_bytes=64)
         d_win = [sb("d_win%d" % t, [P, S], F32) for t in range(PACK)]
         tanh_win = [sb("tanh_win%d" % t, [P, S], F32) for t in range(PACK)]
         for t in range(PACK):
@@ -155,7 +166,6 @@ def tile_picked_hjoingmidcubehopb_none_po_kernel(
             nc.vector.tensor_tensor(lo[:], lo2[:, :, 0], lo2[:, :, 1], ALU.min)
             nc.vector.tensor_tensor(hi[:], hi2[:, :, 0], hi2[:, :, 1], ALU.max)
             nc.vector.tensor_tensor(u[:], lo[:], y_win[t][:, :S], ALU.max)
-            nc.vector.tensor_scalar(d_win[t][:], d_ps[t // 2][:, t % 2, :], gm_t[:, t : t + 1], None, ALU.mult)
             nc.vector.scalar_tensor_tensor(v[:, t, :], hi[:], -0.5, u[:], ALU.mult, ALU.add)
 
         w3w = deal("w3w", w3w_raw, I32)
@@ -177,23 +187,24 @@ def tile_picked_hjoingmidcubehopb_none_po_kernel(
 
         for t in range(PACK):
             nc.scalar.activation(tanh_win[t][:], d_ps[t // 2][:, t % 2, :], ACT.Tanh)
+            nc.scalar.activation(d_win[t][:], d_ps[t // 2][:, t % 2, :], ACT.Copy, scale=gm_t[:, t : t + 1])
         d_n2 = sb("d_n2", [P, PACK, S], F32)
         for t in range(PACK):
             for c in range(2):
                 nc.scalar.activation(d_n2[:, t, c * HALF : (c + 1) * HALF], d_win[t][:].indirect(halves(n2_t, c)), ACT.Copy)
-        prod = sb("prod", [P, PACK, S], F32)
+        prod = keep.tile([P, PACK, S], F32, name="prod", tag="planes", align_bytes=64)
         for b in range(2):
             nc.vector.tensor_tensor(prod[:, 2 * b : 2 * b + 2, :], d_ps[b][:], d_n2[:, 2 * b : 2 * b + 2, :], ALU.mult)
 
         first = psum.tile([P, PACK, HALF], F32, name="h_first", tag="bank0")
-        second = [psum.tile([P, 2, HALF], F32, name="h_second%d" % b, tag="bank%d" % (1 + b)) for b in range(2)]
-        h_ps = [[first[:, t, :] for t in range(PACK)], [second[t // 2][:, t % 2, :] for t in range(PACK)]]
-        per_bank = (4, 2)
+        second = [psum.tile([P, HALF], F32, name="h_second%d" % t, tag="bank%d" % (1, 2, 3, 6)[t]) for t in range(PACK)]
+        h_ps = [[first[:, t, :] for t in range(PACK)], [second[t][:] for t in range(PACK)]]
+        order = (0, 2, 1, 3)
         for c in range(2):
-            for t in range(PACK):
+            for t in order:
                 nc.tensor.matmul_mx(h_ps[c][t], lhsT=w3w[:, cols(t)].bitcast(FP8X4), lhsT_scale=ws[:, cols(t)],
                                     rhs=z_w[:, hcols(c)].bitcast(FP8X4), rhs_scale=z_s[:, hcols(c)],
-                                    start=(t % per_bank[c] == 0), stop=False)
+                                    start=(c == 1 or t == order[0]), stop=False)
         for c in range(2):
             tanh_n3 = sb("tanh_n3_%d" % c, [P, PACK, HALF], F32)
             for t in range(PACK):
@@ -203,28 +214,29 @@ def tile_picked_hjoingmidcubehopb_none_po_kernel(
             z2_w = sb("z2_w%d" % c, [P, HALF], U32)
             z2_s = sb("z2_s%d" % c, [P, HALF], U8)
             nc.vector.quantize_mx(z2_w[:].bitcast(FP8X4), z2_s[:], z2_bf[:])
-            for t in range(PACK):
+            for t in order:
                 nc.tensor.matmul_mx(h_ps[c][t], lhsT=w4w[:, cols(t)].bitcast(FP8X4), lhsT_scale=ws[4:P, cols(t)],
                                     rhs=z2_w[:].bitcast(FP8X4), rhs_scale=z2_s[:],
-                                    start=False, stop=(t % per_bank[c] == per_bank[c] - 1))
+                                    start=False, stop=(c == 1 or t == order[-1]))
 
         h = sb("h", [P, PACK, S], F32)
         nc.scalar.copy(h[:, :, hcols(0)], first[:])
-        nc.scalar.copy(h[:, 0:2, hcols(1)], second[0][:])
-        nc.vector.tensor_copy(h[:, 2:4, hcols(1)], second[1][:])
-        h_n4 = sb("h_n4", [P, PACK, S], F32)
         st = sb("st", [P, PACK, S], F32)
         st_n5 = sb("st_n5", [P, PACK, S], F32)
         res = sb("res", [P, PACK, S], F32)
         out_rows = out_0.rearrange("(p t) j -> p t j", t=PACK)
-        order = (0, 2, 1, 3)
         for t in order:
+            h_n4 = keep.tile([P, S], F32, name="h_n4", tag="h_n4_%d" % (t % 3))
+            if t < 2:
+                nc.scalar.copy(h[:, t, hcols(1)], second[t][:])
+            else:
+                nc.vector.tensor_copy(h[:, t, hcols(1)], second[t][:])
             for c in range(2):
                 if t < 2:
-                    nc.scalar.activation(h_n4[:, t, hcols(c)], h[:, t, :].indirect(halves(n4_t, c)), ACT.Copy)
+                    nc.scalar.activation(h_n4[:, hcols(c)], h[:, t, :].indirect(halves(n4_t, c)), ACT.Copy)
                 else:
-                    nc.vector.tensor_copy(h_n4[:, t, hcols(c)], h[:, t, :].indirect(halves(n4_t, c)))
-            nc.vector.tensor_tensor(st[:, t, :], h_n4[:, t, :], h[:, t, :], ALU.max)
+                    nc.vector.tensor_copy(h_n4[:, hcols(c)], h[:, t, :].indirect(halves(n4_t, c)))
+            nc.vector.tensor_tensor(st[:, t, :], h_n4[:], h[:, t, :], ALU.max)
         for t in order:
             for c in range(2):
                 nc.scalar.activation(st_n5[:, t, hcols(c)], st[:, t, :].indirect(halves(n5_t, c)), ACT.Copy)

@@ -46,13 +46,6 @@ def tile_picked_hjoingmidcubehopb_none_po_kernel(
             queue.dma_start(t[:], words_of(src))
             return t
 
-        def load_first_rows(queue, tile, src):
-            queue.dma_start(tile[0:16, :].bitcast(I32), src[0].bitcast(I32))
-
-        def load_other_rows(queue, tile, src):
-            rows = src[0].bitcast(I32)
-            queue.dma_start(tile[16:P, :].bitcast(I32), rows[2:16, :].unsqueeze(0).to_broadcast([8, 14, rows.shape[1]]))
-
         def deal(name, src, dtype, steps=(PACK,)):
             tile = sb(name, [P, H], dtype)
             run = 4 if dtype == I32 else 16
@@ -70,19 +63,20 @@ def tile_picked_hjoingmidcubehopb_none_po_kernel(
         def halves(lst, c):
             return lst[:, c * (HALF // 16) : (c + 1) * (HALF // 16)]
 
-        def load_scale_rows(queue, tile, first, src):
+        def load_scale_rows(queues, tile, first, src):
             rows = src[0].bitcast(I32)
             for q in range(4):
-                queue.dma_start(tile[32 * q + first : 32 * q + first + 4, :].bitcast(I32), rows[4 * q : 4 * q + 4, :])
+                queues[q].dma_start(tile[32 * q + first : 32 * q + first + 4, :].bitcast(I32), rows[4 * q : 4 * q + 4, :])
 
+        on_sync = [nc.sync] * 4
         xs = sb("xs", [P, T], U8)
         nc.vector.memset(xs[:].bitcast(I32), 0)
         offs_t = load_list("offs_t", offs)
         xw = load_words(nc.sync, "xw", x_words)
-        load_scale_rows(nc.sync, xs, 0, x_scales)
+        load_scale_rows(on_sync, xs, 0, x_scales)
         w1s_raw = sb("w1s_raw", [P, H], U8)
-        load_first_rows(nc.sync, w1s_raw, w1_scales)
-        load_other_rows(nc.sync, w1s_raw, w1_scales)
+        nc.gpsimd.memset(w1s_raw[:].bitcast(I32), 0)
+        load_scale_rows([nc.sync, nc.sync, nc.gpsimd, nc.gpsimd], w1s_raw, 0, w1_scales)
         w1w_raw = load_words(nc.sync, "w1w_raw", w1_words)
         n1_t = load_list("n1_t", n1)
         hz_t = load_list("hz_t", hz)
@@ -101,8 +95,8 @@ def tile_picked_hjoingmidcubehopb_none_po_kernel(
 
         w2w_raw = load_words(nc.sync, "w2w_raw", w2_words)
         w2s_raw = sb("w2s_raw", [P, H], U8)
-        load_first_rows(nc.sync, w2s_raw, w2_scales)
-        load_other_rows(nc.sync, w2s_raw, w2_scales)
+        nc.vector.memset(w2s_raw[:].bitcast(I32), 0)
+        load_scale_rows(on_sync, w2s_raw, 0, w2_scales)
 
         w1s = deal("w1s", w1s_raw, U8, (1, 3))
         w1w = deal("w1w", w1w_raw, I32, (1, 3))
@@ -123,8 +117,8 @@ def tile_picked_hjoingmidcubehopb_none_po_kernel(
         n3_t = load_list("n3_t", n3)
         gn_t = sb("gn_t", [P, PACK], F32)
         nc.sync.dma_start(gn_t[:], gn.rearrange("(p t) o -> p (t o)", t=PACK))
-        load_scale_rows(nc.sync, ws_raw, 0, w3_scales)
-        load_scale_rows(nc.sync, ws_raw, 4, w4_scales)
+        load_scale_rows(on_sync, ws_raw, 0, w3_scales)
+        load_scale_rows(on_sync, ws_raw, 4, w4_scales)
         n4_t = load_list("n4_t", n4)
         n5_t = load_list("n5_t", n5)
 

from contextlib import ExitStack

import concourse.mybir as mybir

K, T, S, N, H, W = 512, 2048, 256, 512, 512, 1024
FLOPS = 4 * 2 * 512 * 512 * 256

F32 = mybir.dt.float32
BF16 = mybir.dt.bfloat16
I32 = mybir.dt.int32
U32 = mybir.dt.uint32
U16 = mybir.dt.uint16
U8 = mybir.dt.uint8
FP8X4 = mybir.dt.float8_e4m3fn_x4
ALU = mybir.AluOpType
ACT = mybir.ActivationFunctionType

P = 128
PACK = 4
HALF = S // 2
Y_WINDOW = W // 2 + 8


def tile_picked_hjoingmidcubehopb_none_po_kernel(
    tc, x_words, x_scales, w1_words, w1_scales, w2_words, w2_scales, gn, gm, w3_words, w3_scales,
    w4_words, w4_scales, offs, hz, n1, n2, n3, n4, n5, out_0, out_1, out_2,
):
    nc = tc.nc
    with ExitStack() as ctx:
        keep = ctx.enter_context(tc.tile_pool(name="keep", bufs=1))
        psum = ctx.enter_context(tc.psum_pool(name="psum", bufs=1))

        def sb(name, shape, dtype):
            return keep.tile(shape, dtype, name=name, align_bytes=64)

        def load_list(name, src):
            t = keep.tile([P, src.shape[1]], U16, name=name)
            nc.sync.dma_start(t[:], src)
            return t

        def words_of(src):
            return src[0].rearrange("p c r -> p (c r)").bitcast(I32)

        def load_words(queue, name, src):
            t = sb(name, [P, src.shape[2]], I32)
            queue.dma_start(t[:], words_of(src))
            return t

        def deal(name, src, dtype, steps=(PACK,)):
            tile = sb(name, [P, H], dtype)
            run = 4 if dtype == I32 else 16
            dst = tile[:].rearrange("p (t c i) -> p c t i", t=PACK, i=run)
            org = src[:].rearrange("p (c i t) -> p c t i", t=PACK, i=run)
            first = 0
            for step in steps:
                nc.vector.tensor_copy(dst[:, :, first : first + step, :], org[:, :, first : first + step, :])
                first = first + step
            return tile

        def hcols(c):
            return slice(c * HALF, (c + 1) * HALF)

        def halves(lst, c):
            return lst[:, c * (HALF // 16) : (c + 1) * (HALF // 16)]

        def load_scale_rows(queues, tile, first, src):
            rows = src[0].bitcast(I32)
            for q in range(4):
                queues[q].dma_start(tile[32 * q + first : 32 * q + first + 4, :].bitcast(I32), rows[4 * q : 4 * q + 4, :])

        on_sync = [nc.sync] * 4
        xs = sb("xs", [P, T], U8)
        nc.vector.memset(xs[:].bitcast(I32), 0)
        offs_t = load_list("offs_t", offs)
        xw = load_words(nc.sync, "xw", x_words)
        load_scale_rows(on_sync, xs, 0, x_scales)
        w1s_raw = sb("w1s_raw", [P, H], U8)
        nc.gpsimd.memset(w1s_raw[:].bitcast(I32), 0)
        load_scale_rows([nc.sync, nc.sync, nc.gpsimd, nc.gpsimd], w1s_raw, 0, w1_scales)
        w1w_raw = load_words(nc.sync, "w1w_raw", w1_words)
        n1_t = load_list("n1_t", n1)
        hz_t = load_list("hz_t", hz)

        xw_offs = sb("xw_offs", [P, S], U32)
        nc.vector.tensor_copy(xw_offs[:], xw[:].bitcast(U32).indirect(offs_t[:]))
        xs_offs = sb("xs_offs", [P, S], U8)
        nc.vector.tensor_copy(xs_offs[:], xs[:].indirect(offs_t[:]))
        for i in range(2):
            nc.sync.dma_start(xs[16 + i : P : 32, :].bitcast(I32), x_scales[0].bitcast(I32)[2 + i : 16 : 4, :])
        ws_raw = sb("ws_raw", [P, H], U8)
        nc.vector.memset(ws_raw[:].bitcast(I32), 0)
        y_win = [sb("y_win%d" % t, [P, Y_WINDOW], F32) for t in range(PACK)]
        for t in range(PACK):
            nc.vector.memset(y_win[t][:, S:], 0.0)

        w2w_raw = load_words(nc.sync, "w2w_raw", w2_words)
        w2s_raw = sb("w2s_raw", [P, H], U8)
        nc.vector.memset(w2s_raw[:].bitcast(I32), 0)
        load_scale_rows(on_sync, w2s_raw, 0, w2_scales)

        w1s = deal("w1s", w1s_raw, U8, (1, 3))
        w1w = deal("w1w", w1w_raw, I32, (1, 3))
        xw_hz = sb("xw_hz", [P, S], U32)
        nc.vector.tensor_copy(xw_hz[:], xw[:].bitcast(U32).indirect(hz_t[:]))
        xs_hz = sb("xs_hz", [P, S], U8)
        nc.vector.tensor_copy(xs_hz[:], xs[:].indirect(hz_t[:]))
        xs_hz_placed = sb("xs_hz_placed", [P, S], U8)
        nc.vector.tensor_copy(xs_hz_placed[:].bitcast(I32), xs_hz[:].bitcast(I32))
        for i in range(2):
            nc.sync.dma_start(xs_hz_placed[2 + i : P : 32, :].bitcast(I32), xs_hz[16 + i : P : 32, :].bitcast(I32))

        gm_t = sb("gm_t", [P, PACK], F32)
        nc.sync.dma_start(gm_t[:], gm.rearrange("(p t) o -> p (t o)", t=PACK))
        w3w_raw = load_words(nc.sync, "w3w_raw", w3_words)
        w4w_raw = load_words(nc.sync, "w4w_raw", w4_words)
        n2_t = load_list("n2_t", n2)
        n3_t = load_list("n3_t", n3)
        gn_t = sb("gn_t", [P, PACK], F32)
        nc.sync.dma_start(gn_t[:], gn.rearrange("(p t) o -> p (t o)", t=PACK))
        load_scale_rows(on_sync, ws_raw, 0, w3_scales)
        load_scale_rows(on_sync, ws_raw, 4, w4_scales)
        n4_t = load_list("n4_t", n4)
        n5_t = load_list("n5_t", n5)

        def cols(t):
            return slice(t * P, (t + 1) * P)

        members = [sb("members%d" % t, [P, S, 4], F32) for t in range(PACK)]
        for t in range(PACK):
            y_ps = psum.tile([P, S], F32, name="y_ps", tag="bank%d" % t)
            nc.tensor.matmul_mx(y_ps[:], lhsT=w1w[:, cols(t)].bitcast(FP8X4), lhsT_scale=w1s[:, cols(t)],
                                rhs=xw_offs[:].bitcast(FP8X4), rhs_scale=xs_offs[:], start=True, stop=True)
            if t < 2:
                nc.scalar.copy(y_win[t][:, :S], y_ps[:])
            else:
                nc.vector.tensor_copy(y_win[t][:, :S], y_ps[:])
            for c in range(2):
                nc.scalar.activation(members[t][:, hcols(c), :].rearrange("p j e -> p (j e)"),
                                     y_win[t][:].indirect(n1_t[:, c * 32 : (c + 1) * 32]), ACT.Copy)

        w2w = deal("w2w", w2w_raw, I32)
        w2s = deal("w2s", w2s_raw, U8)

        d_ps = [psum.tile([P, 2, S], F32, name="d_ps%d" % b, tag="bank%d" % (4 + b)) for b in range(2)]
        for t in range(PACK):
            nc.tensor.matmul_mx(d_ps[t // 2][:, t % 2, :], lhsT=w2w[:, cols(t)].bitcast(FP8X4), lhsT_scale=w2s[:, cols(t)],
                                rhs=xw_hz[:].bitcast(FP8X4), rhs_scale=xs_hz_placed[:], start=True, stop=True)

        v = keep.tile([P, PACK, S], F32, name="v", tag="planes", align_bytes=64)
        d_win = [sb("d_win%d" % t, [P, S], F32) for t in range(PACK)]
        tanh_win = [sb("tanh_win%d" % t, [P, S], F32) for t in range(PACK)]
        for t in range(PACK):
            lo2 = sb("lo2_%d" % t, [P, S, 2], F32)
            hi2 = sb("hi2_%d" % t, [P, S, 2], F32)
            lo = sb("lo_%d" % t, [P, S], F32)
            hi = sb("hi_%d" % t, [P, S], F32)
            u = sb("u_%d" % t, [P, S], F32)
            nc.vector.tensor_tensor(lo2[:], members[t][:, :, 0:2], members[t][:, :, 2:4], ALU.min)
            nc.vector.tensor_tensor(hi2[:], members[t][:, :, 0:2], members[t][:, :, 2:4], ALU.max)
            nc.vector.tensor_tensor(lo[:], lo2[:, :, 0], lo2[:, :, 1], ALU.min)
            nc.vector.tensor_tensor(hi[:], hi2[:, :, 0], hi2[:, :, 1], ALU.max)
            nc.vector.tensor_tensor(u[:], lo[:], y_win[t][:, :S], ALU.max)
            nc.vector.scalar_tensor_tensor(v[:, t, :], hi[:], -0.5, u[:], ALU.mult, ALU.add)

        w3w = deal("w3w", w3w_raw, I32)
        w4w = deal("w4w", w4w_raw, I32)
        ws = deal("ws", ws_raw, U8)

        def woven(ap):
            return ap.rearrange("p (c i t) -> p c t i", i=4, t=PACK)

        def planar(ap):
            return ap.rearrange("p t (c i) -> p c t i", i=4)

        z_bf = sb("z_bf", [P, S * PACK], BF16)
        nc.vector.tensor_tensor(woven(z_bf[:]), planar(v[:]),
                                gn_t[:].unsqueeze(1).unsqueeze(3).to_broadcast([P, S // 4, PACK, 4]), ALU.mult)
        z_w = sb("z_w", [P, S], U32)
        z_s = sb("z_s", [P, S], U8)
        nc.vector.quantize_mx(z_w[:].bitcast(FP8X4), z_s[:], z_bf[:])

        for t in range(PACK):
            nc.scalar.activation(tanh_win[t][:], d_ps[t // 2][:, t % 2, :], ACT.Tanh)
            nc.scalar.activation(d_win[t][:], d_ps[t // 2][:, t % 2, :], ACT.Copy, scale=gm_t[:, t : t + 1])
        d_n2 = sb("d_n2", [P, PACK, S], F32)
        for t in range(PACK):
            for c in range(2):
                nc.scalar.activation(d_n2[:, t, c * HALF : (c + 1) * HALF], d_win[t][:].indirect(halves(n2_t, c)), ACT.Copy)
        prod = keep.tile([P, PACK, S], F32, name="prod", tag="planes", align_bytes=64)
        for b in range(2):
            nc.vector.tensor_tensor(prod[:, 2 * b : 2 * b + 2, :], d_ps[b][:], d_n2[:, 2 * b : 2 * b + 2, :], ALU.mult)

        first = psum.tile([P, PACK, HALF], F32, name="h_first", tag="bank0")
        second = [psum.tile([P, HALF], F32, name="h_second%d" % t, tag="bank%d" % (1, 2, 3, 6)[t]) for t in range(PACK)]
        h_ps = [[first[:, t, :] for t in range(PACK)], [second[t][:] for t in range(PACK)]]
        order = (0, 2, 1, 3)
        for c in range(2):
            for t in order:
                nc.tensor.matmul_mx(h_ps[c][t], lhsT=w3w[:, cols(t)].bitcast(FP8X4), lhsT_scale=ws[:, cols(t)],
                                    rhs=z_w[:, hcols(c)].bitcast(FP8X4), rhs_scale=z_s[:, hcols(c)],
                                    start=(c == 1 or t == order[0]), stop=False)
        for c in range(2):
            tanh_n3 = sb("tanh_n3_%d" % c, [P, PACK, HALF], F32)
            for t in range(PACK):
                nc.scalar.activation(tanh_n3[:, t, :], tanh_win[t][:].indirect(halves(n3_t, c)), ACT.Copy)
            z2_bf = sb("z2_bf%d" % c, [P, HALF * PACK], BF16)
            nc.vector.tensor_tensor(woven(z2_bf[:]), planar(prod[:, :, hcols(c)]), planar(tanh_n3[:]), ALU.mult)
            z2_w = sb("z2_w%d" % c, [P, HALF], U32)
            z2_s = sb("z2_s%d" % c, [P, HALF], U8)
            nc.vector.quantize_mx(z2_w[:].bitcast(FP8X4), z2_s[:], z2_bf[:])
            for t in order:
                nc.tensor.matmul_mx(h_ps[c][t], lhsT=w4w[:, cols(t)].bitcast(FP8X4), lhsT_scale=ws[4:P, cols(t)],
                                    rhs=z2_w[:].bitcast(FP8X4), rhs_scale=z2_s[:],
                                    start=False, stop=(c == 1 or t == order[-1]))

        h = sb("h", [P, PACK, S], F32)
        nc.scalar.copy(h[:, :, hcols(0)], first[:])
        st = sb("st", [P, PACK, S], F32)
        st_n5 = sb("st_n5", [P, PACK, S], F32)
        res = sb("res", [P, PACK, S], F32)
        out_rows = out_0.rearrange("(p t) j -> p t j", t=PACK)
        for t in order:
            h_n4 = keep.tile([P, S], F32, name="h_n4", tag="h_n4_%d" % (t % 3))
            if t < 2:
                nc.scalar.copy(h[:, t, hcols(1)], second[t][:])
            else:
                nc.vector.tensor_copy(h[:, t, hcols(1)], second[t][:])
            for c in range(2):
                if t < 2:
                    nc.scalar.activation(h_n4[:, hcols(c)], h[:, t, :].indirect(halves(n4_t, c)), ACT.Copy)
                else:
                    nc.vector.tensor_copy(h_n4[:, hcols(c)], h[:, t, :].indirect(halves(n4_t, c)))
            nc.vector.tensor_tensor(st[:, t, :], h_n4[:], h[:, t, :], ALU.max)
        for t in order:
            for c in range(2):
                nc.scalar.activation(st_n5[:, t, hcols(c)], st[:, t, :].indirect(halves(n5_t, c)), ACT.Copy)
            pieces = (hcols(0), hcols(1)) if t == order[-1] else (slice(0, S),)
            for piece in pieces:
                nc.vector.scalar_tensor_tensor(res[:, t, piece], h[:, t, piece], -0.5, st_n5[:, t, piece], ALU.mult, ALU.add)
            nc.sync.dma_start(out_rows[:, t, :], res[:, t, :])
        res_w = sb("res_w", [P, S], I32)
        res_s = sb("res_s", [P, S], U8)
        res_bf = [sb("res_bf%d" % c, [P, HALF * PACK], BF16) for c in range(2)]
        for c in range(2):
            nc.vector.tensor_copy(woven(res_bf[c][:]), planar(res[:, :, hcols(c)]))
        for c in range(2):
            nc.vector.quantize_mx(res_w[:, hcols(c)].bitcast(FP8X4), res_s[:, hcols(c)], res_bf[c][:])
            nc.sync.dma_start(words_of(out_1)[:, hcols(c)], res_w[:, hcols(c)])
        for q in range(4):
            queue = nc.scalar if q % 2 == 0 else nc.sync
            queue.dma_start(out_2[0].bitcast(I32)[4 * q : 4 * q + 4, :], res_s[32 * q : 32 * q + 4, :].bitcast(I32))
